import numpy as np
import ml_dtypes


def mxq(x, axis, fmt="e4m3"):
    dtype, down = {"e4m3": (ml_dtypes.float8_e4m3fn, 7), "e5m2": (ml_dtypes.float8_e5m2, 14)}[fmt]
    v = np.moveaxis(np.asarray(x, np.float32).astype(ml_dtypes.bfloat16).astype(np.float64), axis, -1)
    blocks = v.reshape(v.shape[:-1] + (-1, 32))
    amax = np.abs(blocks).max(-1, keepdims=True)
    byte = np.maximum(np.where(amax > 0, np.frexp(amax)[1] - 1 + 127, 0) - down, 1)
    scale = np.exp2(byte - 127.0)
    codes = (blocks / scale).astype(np.float32).astype(dtype).astype(np.float64)
    return np.moveaxis((codes * scale).reshape(v.shape), -1, axis)


WIDE = False


def mx_kscale(k):
    if not WIDE:
        return np.ones(k)
    levels = np.array([10, -10, 5, -5, 0])
    if k % 512:
        return np.exp2(np.random.permutation(np.resize(levels, k // 32))).repeat(32)
    a = np.empty((k // 512, 16))
    for p in range(k // 512):
        a[p, :8] = np.random.permutation(np.resize(levels, 8))
        for g in range(8):
            far = levels[np.abs(levels - a[p, g]) >= 10]
            a[p, g + 8] = far[np.random.randint(len(far))]
    return np.exp2(a.ravel()).repeat(32)


def f64(x):
    return np.asarray(x).astype(np.float64)


def striped(idx):
    return np.tile(idx.reshape(-1, 16).T, (8, 1)).astype(np.uint16)


def unstriped(offs):
    return offs[:16].T.reshape(-1).astype(np.int64)


def pack_weight(w):
    k, n = w.shape
    w = f64(np.asarray(w, np.float32).astype(ml_dtypes.bfloat16)).reshape(k // 32, 32, n)
    amax = np.abs(w).max(1)
    byte = np.clip(np.where(amax > 0, np.frexp(amax)[1] - 1 + 127 - 7, 1), 1, 254)
    scaled = (w * np.exp2(127.0 - byte)[:, None, :]).reshape(k, n).astype(np.float32)
    words = np.ascontiguousarray(scaled.reshape(k // 512, 128, 4, n).transpose(0, 1, 3, 2)).astype(ml_dtypes.float8_e4m3fn).view(np.uint8)
    return words, np.ascontiguousarray(byte.astype(np.uint8).reshape(k // 512, 16, n))


def unpack_weight(words, scales):
    g, p, n, _ = words.shape
    vals = np.ascontiguousarray(words).view(ml_dtypes.float8_e4m3fn).astype(np.float64) * np.repeat(np.exp2(scales.astype(np.float64) - 127.0), 8, axis=1)[..., None]
    return vals.transpose(0, 1, 3, 2).reshape(g * 512, n)


K, T, D, S, V, N = 1536, 1024, 3, 512, 256, 128


def setup_inputs():
    n = np.random.standard_normal
    s = mx_kscale(K)[:, None]
    words, scales = pack_weight(n((K, N)) / np.sqrt(K) / s)
    return {
        "xT": (n((K, T)) * s).astype(np.float32),
        "w_words": words,
        "w_scales": scales,
        "gate": np.tile(np.random.uniform(0.2, 1.0, (D, 1, V)) / np.sqrt(D), (1, N, 1)).astype(np.float32),
        "offs": striped(np.random.permutation(T)[:S]),
        "pos1": striped(np.random.permutation(S)[:V]),
        "pos2": striped(np.random.permutation(S)[:V]),
        "pos3": striped(np.random.permutation(S)[:V]),
    }


def reference(xT, w_words, w_scales, gate, offs, pos1, pos2, pos3):
    w = unpack_weight(w_words, w_scales)
    idx = unstriped(offs)
    xq = mxq(f64(xT)[:, idx], 0, "e4m3")
    y = w.T @ xq
    return sum(f64(gate[d]) * y[:, unstriped(p)] for d, p in enumerate((pos1, pos2, pos3)))

@@ -1,0 +1,130 @@
+from contextlib import ExitStack
+
+import concourse.mybir as mybir
+
+K, T, D, S, V, N = 1536, 1024, 3, 512, 256, 128
+
+F32 = mybir.dt.float32
+BF16 = mybir.dt.bfloat16
+I32 = mybir.dt.int32
+U32 = mybir.dt.uint32
+U16 = mybir.dt.uint16
+U8 = mybir.dt.uint8
+FP8X4 = mybir.dt.float8_e4m3fn_x4
+ADD = mybir.AluOpType.add
+MULT = mybir.AluOpType.mult
+
+FLOPS = 2 * K * S * N + 5 * V * N
+
+P = 128
+PACK = 4
+K_PASS = P * PACK
+PASSES = K // K_PASS
+
+CHUNKS = {
+    (0, 0): ((0, 352, 512), (512, 864, 1024)),
+    (0, 1): ((0, 352, 512), (512, 864, 1024)),
+    (1, 0): ((0, 352, 512), (512, 864, 1024)),
+    (1, 1): ((0, 352, 512), (512, 864, 1024)),
+    (2, 0): ((0, 352, 512), (512, 864, 1024)),
+    (2, 1): ((0, 352, 512), (512, 768, 896), (896, 896, 1024)),
+}
+PARTS = ((0, 256), (256, 384), (384, 512))
+
+
+def tile_picked_sub_lin_none_sub_e_kernel(
+    tc, xT, w_words, w_scales, gate, offs, pos1, pos2, pos3, out
+):
+    nc = tc.nc
+    with ExitStack() as ctx:
+        held = ctx.enter_context(tc.tile_pool(name="held", bufs=1))
+        psum = ctx.enter_context(tc.psum_pool(name="psum", bufs=1))
+
+        lists = [held.tile([P, src.shape[1]], U16, name=f"list{i}") for i, src in enumerate((offs, pos1, pos2, pos3))]
+        w_codes = held.tile([P, PASSES, N], U32, align_bytes=64, name="w_codes")
+        w_planes = held.tile([P, PASSES, N], U8, align_bytes=64, name="w_planes")
+        gates = held.tile([P, D, V], F32, name="gates")
+
+        nc.gpsimd.memset(w_planes[:].rearrange("p a m -> p (a m)").bitcast(I32), 0)
+
+        raw = {}
+        for a, u in CHUNKS:
+            rows = xT[a * K_PASS : (a + 1) * K_PASS, :].rearrange("(p j) t -> p j t", j=PACK)
+            for t0, unused, t1 in CHUNKS[a, u]:
+                tile = held.tile([P, 2, t1 - t0], F32, name=f"raw_{a}_{u}_{t0}")
+                nc.sync.dma_start(out=tile[:], in_=rows[:, 2 * u : 2 * u + 2, t0:t1])
+                raw[a, u, t0] = tile
+            if (a, u) == (0, 0):
+                nc.sync.dma_start(out=lists[0][:], in_=offs)
+        nc.sync.dma_start(
+            out=w_codes[:].bitcast(I32), in_=w_words.rearrange("a p m r -> p a (m r)").bitcast(I32)
+        )
+        for q in range(4):
+            nc.sync.dma_start(
+                out=w_planes[32 * q : 32 * q + 4, :, :].bitcast(I32),
+                in_=w_scales[:, 4 * q : 4 * q + 4, :].rearrange("a q m -> q a m").bitcast(I32),
+            )
+        nc.sync.dma_start(out=gates[:], in_=gate.rearrange("d m v -> m d v"))
+        for i, src in enumerate((pos1, pos2, pos3)):
+            nc.sync.dma_start(out=lists[1 + i][:], in_=src)
+
+        banks = [psum.tile([N, s1 - s0], F32, name=f"bank_{s0}") for s0, s1 in PARTS]
+        y = held.tile([N, S], F32, name="y")
+
+        def cast(a, u, pairs):
+            for t0, ts, t1 in CHUNKS[a, u]:
+                src = raw[a, u, t0][:].rearrange("p e t -> p t e")
+                if ts > t0:
+                    nc.scalar.copy(out=pairs[:, t0:ts, :], in_=src[:, 0 : ts - t0, :])
+                nc.vector.tensor_copy(out=pairs[:, ts:t1, :], in_=src[:, ts - t0 : t1 - t0, :])
+
+        def product(a, codes, planes, part):
+            s0, s1 = PARTS[part]
+            nc.tensor.matmul_mx(
+                out=banks[part][:],
+                lhsT=w_codes[:, a, :].bitcast(FP8X4),
+                lhsT_scale=w_planes[:, a, :],
+                rhs=codes[:, s0:s1].bitcast(FP8X4),
+                rhs_scale=planes[:, s0:s1],
+                start=(a == 0),
+                stop=(a == PASSES - 1),
+            )
+
+        for a in range(PASSES):
+            last = a == PASSES - 1
+            picked = held.tile([P, S, PACK], BF16, align_bytes=64, name=f"picked{a}")
+            codes = held.tile([P, S], U32, align_bytes=64, name=f"codes{a}")
+            planes = held.tile([P, S], U8, align_bytes=64, name=f"planes{a}")
+            flat = picked[:].rearrange("p s j -> p (s j)")
+            words = flat.bitcast(U32).rearrange("p (s u) -> p s u", u=2)
+            for u in range(2):
+                pairs = held.tile([P, T, 2], BF16, align_bytes=64, name=f"pairs_{a}_{u}")
+                cast(a, u, pairs)
+                window = pairs[:].rearrange("p t e -> p (t e)").bitcast(U32)
+                for s0, s1 in ((0, 256), (256, 512)) if last and u == 1 else ((0, S),):
+                    nc.vector.tensor_copy(
+                        out=words[:, s0:s1, u], in_=window.indirect(lists[0][:, s0 // 16 : s1 // 16])
+                    )
+            for s0, s1 in PARTS if last else ((0, S),):
+                nc.vector.quantize_mx(
+                    out=codes[:, s0:s1].bitcast(FP8X4),
+                    scales=planes[:, s0:s1],
+                    in_=flat[:, PACK * s0 : PACK * s1],
+                )
+            for part in range(len(PARTS)):
+                product(a, codes, planes, part)
+
+        nc.scalar.copy(out=y[:, 0:256], in_=banks[0][:])
+        nc.vector.tensor_copy(out=y[:, 256:384], in_=banks[1][:])
+        nc.scalar.copy(out=y[:, 384:512], in_=banks[2][:])
+
+        terms = []
+        for d in range(D):
+            term = held.tile([N, V], F32, name=f"term{d}")
+            nc.vector.tensor_tensor(out=term[:], in0=y[:].indirect(lists[1 + d][:]), in1=gates[:, d, :], op=MULT)
+            terms.append(term)
+        first = held.tile([N, V], F32, name="first")
+        total = held.tile([N, V], F32, name="total")
+        nc.vector.tensor_tensor(out=first[:], in0=terms[0][:], in1=terms[1][:], op=ADD)
+        nc.vector.tensor_tensor(out=total[:], in0=first[:], in1=terms[2][:], op=ADD)
+        nc.sync.dma_start(out=out, in_=total[:])

@@ -22,12 +22,12 @@ K_PASS = P * PACK
 PASSES = K // K_PASS
 
 CHUNKS = {
-    (0, 0): ((0, 352, 512), (512, 864, 1024)),
-    (0, 1): ((0, 352, 512), (512, 864, 1024)),
-    (1, 0): ((0, 352, 512), (512, 864, 1024)),
-    (1, 1): ((0, 352, 512), (512, 864, 1024)),
-    (2, 0): ((0, 352, 512), (512, 864, 1024)),
-    (2, 1): ((0, 352, 512), (512, 768, 896), (896, 896, 1024)),
+    (0, 0): ((0, 320, 384, 384), (384, 864, 1024, 1024)),
+    (0, 1): ((0, 832, 1024, 1024),),
+    (1, 0): ((0, 832, 1024, 1024),),
+    (1, 1): ((0, 736, 1024, 1024),),
+    (2, 0): ((0, 352, 512, 512), (512, 864, 1024, 1024)),
+    (2, 1): ((0, 352, 512, 512), (512, 656, 656, 768), (768, 896, 896, 1024)),
 }
 PARTS = ((0, 256), (256, 384), (384, 512))
 
@@ -50,7 +50,8 @@ def tile_picked_sub_lin_none_sub_e_kernel(
         raw = {}
         for a, u in CHUNKS:
             rows = xT[a * K_PASS : (a + 1) * K_PASS, :].rearrange("(p j) t -> p j t", j=PACK)
-            for t0, unused, t1 in CHUNKS[a, u]:
+            for chunk in CHUNKS[a, u]:
+                t0, t1 = chunk[0], chunk[-1]
                 tile = held.tile([P, 2, t1 - t0], F32, name=f"raw_{a}_{u}_{t0}")
                 nc.sync.dma_start(out=tile[:], in_=rows[:, 2 * u : 2 * u + 2, t0:t1])
                 raw[a, u, t0] = tile
@@ -72,11 +73,17 @@ def tile_picked_sub_lin_none_sub_e_kernel(
         y = held.tile([N, S], F32, name="y")
 
         def cast(a, u, pairs):
-            for t0, ts, t1 in CHUNKS[a, u]:
+            for chunk in CHUNKS[a, u]:
+                t0 = chunk[0]
                 src = raw[a, u, t0][:].rearrange("p e t -> p t e")
-                if ts > t0:
-                    nc.scalar.copy(out=pairs[:, t0:ts, :], in_=src[:, 0 : ts - t0, :])
-                nc.vector.tensor_copy(out=pairs[:, ts:t1, :], in_=src[:, ts - t0 : t1 - t0, :])
+                for engine, b0, b1 in zip(("scalar", "gpsimd", "vector"), chunk, chunk[1:]):
+                    dst, part = pairs[:, b0:b1, :], src[:, b0 - t0 : b1 - t0, :]
+                    if b1 > b0 and engine == "scalar":
+                        nc.scalar.copy(out=dst, in_=part)
+                    elif b1 > b0 and engine == "gpsimd":
+                        nc.gpsimd.tensor_scalar(out=dst, in0=part, scalar1=1.0, scalar2=0.0, op0=MULT, op1=ADD)
+                    elif b1 > b0:
+                        nc.vector.tensor_copy(out=dst, in_=part)
 
         def product(a, codes, planes, part):
             s0, s1 = PARTS[part]

from contextlib import ExitStack

import concourse.mybir as mybir

K, T, D, S, V, N = 1536, 1024, 3, 512, 256, 128

F32 = mybir.dt.float32
BF16 = mybir.dt.bfloat16
I32 = mybir.dt.int32
U32 = mybir.dt.uint32
U16 = mybir.dt.uint16
U8 = mybir.dt.uint8
FP8X4 = mybir.dt.float8_e4m3fn_x4
ADD = mybir.AluOpType.add
MULT = mybir.AluOpType.mult

FLOPS = 2 * K * S * N + 5 * V * N

P = 128
PACK = 4
K_PASS = P * PACK
PASSES = K // K_PASS

CHUNKS = {
    (0, 0): ((0, 320, 384, 384), (384, 864, 1024, 1024)),
    (0, 1): ((0, 832, 1024, 1024),),
    (1, 0): ((0, 832, 1024, 1024),),
    (1, 1): ((0, 736, 1024, 1024),),
    (2, 0): ((0, 352, 512, 512), (512, 864, 1024, 1024)),
    (2, 1): ((0, 352, 512, 512), (512, 656, 656, 768), (768, 896, 896, 1024)),
}
PARTS = ((0, 256), (256, 384), (384, 512))


def tile_picked_sub_lin_none_sub_e_kernel(
    tc, xT, w_words, w_scales, gate, offs, pos1, pos2, pos3, out
):
    nc = tc.nc
    with ExitStack() as ctx:
        held = ctx.enter_context(tc.tile_pool(name="held", bufs=1))
        psum = ctx.enter_context(tc.psum_pool(name="psum", bufs=1))

        lists = [held.tile([P, src.shape[1]], U16, name=f"list{i}") for i, src in enumerate((offs, pos1, pos2, pos3))]
        w_codes = held.tile([P, PASSES, N], U32, align_bytes=64, name="w_codes")
        w_planes = held.tile([P, PASSES, N], U8, align_bytes=64, name="w_planes")
        gates = held.tile([P, D, V], F32, name="gates")

        nc.gpsimd.memset(w_planes[:].rearrange("p a m -> p (a m)").bitcast(I32), 0)

        raw = {}
        for a, u in CHUNKS:
            rows = xT[a * K_PASS : (a + 1) * K_PASS, :].rearrange("(p j) t -> p j t", j=PACK)
            for chunk in CHUNKS[a, u]:
                t0, t1 = chunk[0], chunk[-1]
                tile = held.tile([P, 2, t1 - t0], F32, name=f"raw_{a}_{u}_{t0}")
                nc.sync.dma_start(out=tile[:], in_=rows[:, 2 * u : 2 * u + 2, t0:t1])
                raw[a, u, t0] = tile
            if (a, u) == (0, 0):
                nc.sync.dma_start(out=lists[0][:], in_=offs)
        nc.sync.dma_start(
            out=w_codes[:].bitcast(I32), in_=w_words.rearrange("a p m r -> p a (m r)").bitcast(I32)
        )
        for q in range(4):
            nc.sync.dma_start(
                out=w_planes[32 * q : 32 * q + 4, :, :].bitcast(I32),
                in_=w_scales[:, 4 * q : 4 * q + 4, :].rearrange("a q m -> q a m").bitcast(I32),
            )
        nc.sync.dma_start(out=gates[:], in_=gate.rearrange("d m v -> m d v"))
        for i, src in enumerate((pos1, pos2, pos3)):
            nc.sync.dma_start(out=lists[1 + i][:], in_=src)

        banks = [psum.tile([N, s1 - s0], F32, name=f"bank_{s0}") for s0, s1 in PARTS]
        y = held.tile([N, S], F32, name="y")

        def cast(a, u, pairs):
            for chunk in CHUNKS[a, u]:
                t0 = chunk[0]
                src = raw[a, u, t0][:].rearrange("p e t -> p t e")
                for engine, b0, b1 in zip(("scalar", "gpsimd", "vector"), chunk, chunk[1:]):
                    dst, part = pairs[:, b0:b1, :], src[:, b0 - t0 : b1 - t0, :]
                    if b1 > b0 and engine == "scalar":
                        nc.scalar.copy(out=dst, in_=part)
                    elif b1 > b0 and engine == "gpsimd":
                        nc.gpsimd.tensor_scalar(out=dst, in0=part, scalar1=1.0, scalar2=0.0, op0=MULT, op1=ADD)
                    elif b1 > b0:
                        nc.vector.tensor_copy(out=dst, in_=part)

        def product(a, codes, planes, part):
            s0, s1 = PARTS[part]
            nc.tensor.matmul_mx(
                out=banks[part][:],
                lhsT=w_codes[:, a, :].bitcast(FP8X4),
                lhsT_scale=w_planes[:, a, :],
                rhs=codes[:, s0:s1].bitcast(FP8X4),
                rhs_scale=planes[:, s0:s1],
                start=(a == 0),
                stop=(a == PASSES - 1),
            )

        for a in range(PASSES):
            last = a == PASSES - 1
            picked = held.tile([P, S, PACK], BF16, align_bytes=64, name=f"picked{a}")
            codes = held.tile([P, S], U32, align_bytes=64, name=f"codes{a}")
            planes = held.tile([P, S], U8, align_bytes=64, name=f"planes{a}")
            flat = picked[:].rearrange("p s j -> p (s j)")
            words = flat.bitcast(U32).rearrange("p (s u) -> p s u", u=2)
            for u in range(2):
                pairs = held.tile([P, T, 2], BF16, align_bytes=64, name=f"pairs_{a}_{u}")
                cast(a, u, pairs)
                window = pairs[:].rearrange("p t e -> p (t e)").bitcast(U32)
                for s0, s1 in ((0, 256), (256, 512)) if last and u == 1 else ((0, S),):
                    nc.vector.tensor_copy(
                        out=words[:, s0:s1, u], in_=window.indirect(lists[0][:, s0 // 16 : s1 // 16])
                    )
            for s0, s1 in PARTS if last else ((0, S),):
                nc.vector.quantize_mx(
                    out=codes[:, s0:s1].bitcast(FP8X4),
                    scales=planes[:, s0:s1],
                    in_=flat[:, PACK * s0 : PACK * s1],
                )
            for part in range(len(PARTS)):
                product(a, codes, planes, part)

        nc.scalar.copy(out=y[:, 0:256], in_=banks[0][:])
        nc.vector.tensor_copy(out=y[:, 256:384], in_=banks[1][:])
        nc.scalar.copy(out=y[:, 384:512], in_=banks[2][:])

        terms = []
        for d in range(D):
            term = held.tile([N, V], F32, name=f"term{d}")
            nc.vector.tensor_tensor(out=term[:], in0=y[:].indirect(lists[1 + d][:]), in1=gates[:, d, :], op=MULT)
            terms.append(term)
        first = held.tile([N, V], F32, name="first")
        total = held.tile([N, V], F32, name="total")
        nc.vector.tensor_tensor(out=first[:], in0=terms[0][:], in1=terms[1][:], op=ADD)
        nc.vector.tensor_tensor(out=total[:], in0=first[:], in1=terms[2][:], op=ADD)
        nc.sync.dma_start(out=out, in_=total[:])
